import numpy as np, ml_dtypes
CORES = [24,40,56,80,88,96]
N = 6
import mx_ref
NC, G, MB, ROOT = 256, 4, 2, 3
C = np.float32(0.019)
BF = ml_dtypes.bfloat16
def cut(t, i, w=512):
    return t[:, w * i:w * i + w]
def tile(rs):
    return np.stack(rs, axis=2).reshape(128, -1).astype(BF)
def layer(w, X):
    out = []
    for i in range(G):
        for t in range(len(X)):
            p = mx_ref.matmul(mx_ref.quantize(cut(w, len(X) * i + t)), X[t])
            z = p if t == 0 else z + p
        out.append(z)
    return out
def act(Z):
    return [np.maximum(z, 0) * C for z in Z]
def setup_inputs(rng):
    def f(*shape):
        return mx_ref.flush((rng.standard_normal(shape, dtype=np.float32) * np.exp2(rng.integers(-2, 3, shape[:-1] + (1,)))).astype(BF))
    return {"x": f(N, 128, MB * 4 * NC), "w1": f(N, 128, G * 512), "w2": f(N, 128, 512)}
def setup_inputs_blocks(rng):
    d = setup_inputs(rng)
    for k in ("x", "w1", "w2"): d[k] = mx_ref.spread(d[k], rng, 4)
    return d
def setup_inputs_wide(rng):
    d = setup_inputs(rng)
    for k in ("x", "w1", "w2"): d[k] = mx_ref.flush((d[k].astype(np.float32) * np.exp2(rng.integers(-8, 9, (N, 1, 1))).astype(np.float32)).astype(BF))
    return d
def setup_inputs_zeros(rng):
    d = setup_inputs(rng); v = d["x"].reshape(N, 128, -1, 4).copy()
    v[np.broadcast_to((rng.random((N, 1, v.shape[2], 1)) < 0.33), v.shape)] = 0
    d["x"] = v.reshape(d["x"].shape)
    return d
def reference(x, w1, w2):
    H = [mx_ref.quantize(tile(act(layer(w1[ROOT], [mx_ref.quantize(cut(x[ROOT], m, 4 * NC))])))) for m in range(MB)]
    y = np.zeros((N, 128, MB * NC), np.float32)
    for r in range(N):
        qw = mx_ref.quantize(w2[r])
        for m in range(MB):
            y[r][:, NC * m:NC * m + NC] = mx_ref.matmul(qw, H[m])
    return {"y": y}

@@ -1,0 +1,209 @@
+from concourse.bass import DstId, RemoteDMATransfer
+from concourse.mybir import dt, AluOpType, ActivationFunctionType
+
+SCRATCH = {
+    "xt": ("sbuf", [128, 2048], "bfloat16"),
+    "wt": ("sbuf", [128, 2048], "bfloat16"),
+    "w2t": ("sbuf", [128, 512], "bfloat16"),
+    "xq": ("sbuf", [128, 512], "float8_e4m3fn_x4"),
+    "xs": ("sbuf", [128, 512], "uint8"),
+    "wq": ("sbuf", [128, 512], "float8_e4m3fn_x4"),
+    "ws": ("sbuf", [128, 512], "uint8"),
+    "w2q": ("sbuf", [128, 128], "float8_e4m3fn_x4"),
+    "w2s": ("sbuf", [128, 128], "uint8"),
+    "h": ("sbuf", [128, 2048], "bfloat16"),
+    "hq": ("sbuf", [128, 512], "float8_e4m3fn_x4"),
+    "hs": ("sbuf", [128, 512], "uint8"),
+    "yt": ("sbuf", [128, 512], "float32"),
+    "z": ("psum", [128, 4096], "float32"),
+}
+SEMAPHORES = ["lx0", "lx1", "lx2", "lw0", "lw1", "lw2", "vec", "ten", "act", "st0", "st1", "st2",
+              "pa", "pb", "c0", "c1", "sent"]
+C = 0.019
+CORES_SIMULATED = 112
+PIECES = {"pa": ("hs", 0, 128, 0), "c0": ("hq", 0, 256, 1), "c1": ("hq", 256, 512, 3), "pb": ("hs", 128, 512, 3)}
+
+
+def bits(mask):
+    return bin(mask).count("1")
+
+
+def low(mask, n):
+    out = 0
+    for e in range(16):
+        if mask >> e & 1 and bits(out) < n:
+            out |= 1 << e
+    return out
+
+
+def routes(T, topo):
+    root = T.cores[T.root]
+    others = [c for c in T.cores if c != root]
+    plane = [c for c in others if topo.may_write(root, c)]
+    far = [c for c in others if not topo.may_write(root, c)]
+    mate = [c for c in far if topo.mates(topo.chip(root), topo.chip(c))]
+    r = [c for c in far if c not in mate]
+    ports = [c for c in range(CORES_SIMULATED) if c != root and topo.chip(c) == topo.chip(root)
+             and all(topo.may_write(c, d) for d in others)]
+    a0, a1 = [c for c in ports if topo.die(c) == topo.die(root)][:2]
+    b0, b1 = [c for c in ports if topo.die(c) != topo.die(root)][:2]
+    m, p = mate[0], plane[0]
+    off = low(topo.mask(root, p), 8)
+    chip = topo.mask(root, a0)
+    rest = chip & ~off
+    return {
+        root: [("pa", off, [a0, a1, b0, b1]), ("c0", rest, [a0, b0]), ("c1", chip, [a1, b1]),
+               ("pb", chip, [a0, b0]), ("c0", off, [p])],
+        a0: [("pa", off, [m]), ("c0", off, [m, r[0]]), ("pb", off, [r[1], r[2], p])],
+        b0: [("pa", off, [r[1]]), ("c0", off, [r[1], r[2]]), ("pb", off, [m, r[0]])],
+        a1: [("pa", off, [r[2], p]), ("c1", off, [r[1], r[2], p])],
+        b1: [("pa", off, [r[0]]), ("c1", off, [r[0], m])],
+    }
+
+
+def view(T, piece):
+    buf, a, b, last = PIECES[piece]
+    return T.hq[:, a:b].bitcast(dt.uint8) if buf == "hq" else T.hs[:, a:b]
+
+
+def send(g, T, topo, calls, ready):
+    total = 0
+    seen = []
+    for piece, mask, dests in calls:
+        if piece not in seen:
+            seen.append(piece)
+            ready(piece)
+        ids = []
+        for d in dests:
+            rid, pid, _se = topo.addr(d)
+            ids.append(DstId(rid=rid, pnc=pid))
+        g.remote_dma_fused([RemoteDMATransfer(dst_ids=ids, dma_engine_mask=mask, remote_sem=T.sem[piece],
+                                              srcs=[view(T, piece)], dsts=[view(T, piece) for _ in dests])],
+                           local_sem=T.sem.sent)
+        total += bits(mask)
+    g.wait_ge(T.sem.sent, total)
+
+
+def queue(eng, sem):
+    n = [0]
+
+    def do(ins):
+        n[0] += 1
+        ins.then_inc(sem, 1)
+        return n[0]
+    return do
+
+
+def output(g, T, vdo, tdo, sdo, w2_ready, h_ready, free):
+    S = T.sem
+    cp = [0] * 4
+    g.tensor.wait_ge(S.vec, w2_ready)
+    for u in range(4):
+        h_ready(u)
+        free(u)
+        k = tdo(g.tensor.matmul_mx(T.z[:, 512 * u:512 * u + 128], T.w2q[:, 0:128], T.w2s[:, 0:128],
+                                   T.hq[:, 128 * u:128 * u + 128], T.hs[:, 128 * u:128 * u + 128], True, True))
+        src, dst = T.z[:, 512 * u:512 * u + 128], T.yt[:, 128 * u:128 * u + 128]
+        if u % 2 == 0:
+            g.vector.wait_ge(S.ten, k)
+            cp[u] = vdo(g.vector.tensor_copy(dst, src))
+        else:
+            g.scalar.wait_ge(S.ten, k)
+            cp[u] = sdo(g.scalar.activation(dst, src, ActivationFunctionType.Copy))
+    g.sync.wait_ge(S.vec, cp[0])
+    g.sync.dma_start(T.y[:, 0:128], T.yt[:, 0:128]).then_inc(S.st0, 16)
+    g.sync.wait_ge(S.act, cp[1])
+    g.sync.wait_ge(S.vec, cp[2])
+    g.sync.dma_start(T.y[:, 128:384], T.yt[:, 128:384]).then_inc(S.st1, 16)
+    g.scalar.wait_ge(S.act, cp[3])
+    g.scalar.dma_start(T.y[:, 384:512], T.yt[:, 384:512]).then_inc(S.st2, 16)
+    g.sync.wait_ge(S.st0, 16)
+    g.sync.wait_ge(S.st1, 16)
+    g.scalar.wait_ge(S.st2, 16)
+
+
+def root_program(g, T, topo, calls):
+    S = T.sem
+    vdo, tdo, sdo = queue(g.vector, S.vec), queue(g.tensor, S.ten), queue(g.scalar, S.act)
+    g.sync.dma_start(T.xt[:, 0:512], T.x[:, 0:512]).then_inc(S.lx0, 16)
+    g.scalar.dma_start(T.wt[:, 0:1024], T.w1[:, 0:1024]).then_inc(S.lw0, 16)
+    g.sync.dma_start(T.wt[:, 1024:2048], T.w1[:, 1024:2048]).then_inc(S.lw1, 16)
+    g.scalar.dma_start(T.xt[:, 512:1024], T.x[:, 512:1024]).then_inc(S.lx1, 16)
+    g.sync.dma_start(T.xt[:, 1024:2048], T.x[:, 1024:2048]).then_inc(S.lx2, 16)
+    g.scalar.dma_start(T.w2t[:], T.w2[:]).then_inc(S.lw2, 16)
+
+    def quant(q, s, t, k):
+        return vdo(g.vector.quantize_mx(q[:, 128 * k:128 * k + 128], s[:, 128 * k:128 * k + 128],
+                                        t[:, 512 * k:512 * k + 512]))
+
+    xk, wk, hk = [0] * 4, [0] * 4, [0] * 4
+    g.vector.wait_ge(S.lx0, 16)
+    xk[0] = quant(T.xq, T.xs, T.xt, 0)
+    for i in range(4):
+        if i % 2 == 0:
+            g.vector.wait_ge(S.lw1 if i else S.lw0, 16)
+        wk[i] = quant(T.wq, T.ws, T.wt, i)
+    done = {}
+    for u in range(4):
+        if u == 1:
+            g.vector.wait_ge(S.lx1, 16)
+            xk[1] = quant(T.xq, T.xs, T.xt, 1)
+        if u == 2:
+            g.vector.wait_ge(S.lx2, 16)
+            xk[2] = quant(T.xq, T.xs, T.xt, 2)
+            xk[3] = quant(T.xq, T.xs, T.xt, 3)
+        for i in range(4):
+            bank = 4 * (u % 2) + i
+            g.tensor.wait_ge(S.vec, max(xk[u], wk[i]))
+            if u >= 2:
+                g.tensor.wait_ge(*done[(u - 2, i)])
+            k = tdo(g.tensor.matmul_mx(T.z[:, 512 * bank:512 * bank + 128],
+                                       T.wq[:, 128 * i:128 * i + 128], T.ws[:, 128 * i:128 * i + 128],
+                                       T.xq[:, 128 * u:128 * u + 128], T.xs[:, 128 * u:128 * u + 128], True, True))
+            src = T.z[:, 512 * bank:512 * bank + 128]
+            dst = T.h[:, 512 * u + i:512 * u + 512:4]
+            if i % 2 == 0:
+                g.scalar.wait_ge(S.ten, k)
+                done[(u, i)] = (S.act, sdo(g.scalar.activation(dst, src, ActivationFunctionType.Relu, scale=C)))
+            else:
+                g.vector.wait_ge(S.ten, k)
+                done[(u, i)] = (S.vec, vdo(g.vector.tensor_scalar(dst, src, 0.0, C, AluOpType.max, AluOpType.mult)))
+        g.vector.wait_ge(*done[(u, 2)])
+        g.vector.wait_ge(*done[(u, 3)])
+        hk[u] = quant(T.hq, T.hs, T.h, u)
+    g.vector.wait_ge(S.lw2, 16)
+    w2k = vdo(g.vector.quantize_mx(T.w2q[:, 0:128], T.w2s[:, 0:128], T.w2t[:, 0:512]))
+
+    def free(u):
+        g.tensor.wait_ge(*done[(2, u)])
+    output(g, T, vdo, tdo, sdo, w2k, lambda u: g.tensor.wait_ge(S.vec, hk[u]), free)
+    send(g, T, topo, calls, lambda piece: g.wait_ge(S.vec, hk[PIECES[piece][3]]))
+
+
+def rank_program(g, core, T, topo):
+    R = routes(T, topo)
+    rank = T.rank_of(core)
+    calls = R[core] if core in R else []
+    if rank is not None and rank == T.root:
+        root_program(g, T, topo, calls)
+        return
+    S = T.sem
+    arrives = {}
+    for src in R:
+        for piece, mask, dests in R[src]:
+            if core in dests:
+                arrives[piece] = bits(mask)
+    if calls:
+        send(g, T, topo, calls, lambda piece: g.wait_ge(S[piece], arrives[piece]))
+    if rank is None:
+        return
+    vdo, tdo, sdo = queue(g.vector, S.vec), queue(g.tensor, S.ten), queue(g.scalar, S.act)
+    g.sync.dma_start(T.w2t[:], T.w2[:]).then_inc(S.lw2, 16)
+    g.vector.wait_ge(S.lw2, 16)
+    w2k = vdo(g.vector.quantize_mx(T.w2q[:, 0:128], T.w2s[:, 0:128], T.w2t[:, 0:512]))
+    need = [["pa", "c0"], ["pb"], ["c1"], []]
+
+    def h_ready(u):
+        for piece in need[u]:
+            g.tensor.wait_ge(S[piece], arrives[piece])
+    output(g, T, vdo, tdo, sdo, w2k, h_ready, lambda u: None)

@@ -17,11 +17,14 @@ SCRATCH = {
     "yt": ("sbuf", [128, 512], "float32"),
     "z": ("psum", [128, 4096], "float32"),
 }
-SEMAPHORES = ["lx0", "lx1", "lx2", "lw0", "lw1", "lw2", "vec", "ten", "act", "st0", "st1", "st2",
-              "pa", "pb", "c0", "c1", "sent"]
+PIECES = {"u0": ("hq", 0, 1), "u1": ("hq", 1, 2), "u2": ("hq", 2, 3), "u3": ("hq", 3, 4), "pl": ("hs", 0, 4)}
+LOADED = {"x0": "lx0", "x1": "lx1", "x2": "lx2", "x3": "lx2", "w0": "lw0", "w1": "lw0", "w2": "lw2", "w3": "lw3"}
+SEMAPHORES = ["lx0", "lx1", "lx2", "lw0", "lw2", "lw3", "lv", "vec", "ten", "act", "st0", "st1", "st2",
+              "sent"] + list(PIECES)
+VECTOR = ["x0", "w0", "w1", "w2", "w3", "z01", "x1", "z03", "h0", "x2", "x3", "z10", "z13", "h1",
+          "z21", "z23", "h2", "z31", "z33", "h3"]
 C = 0.019
 CORES_SIMULATED = 112
-PIECES = {"pa": ("hs", 0, 128, 0), "c0": ("hq", 0, 256, 1), "c1": ("hq", 256, 512, 3), "pb": ("hs", 128, 512, 3)}
 
 
 def bits(mask):
@@ -39,31 +42,39 @@ def low(mask, n):
 def routes(T, topo):
     root = T.cores[T.root]
     others = [c for c in T.cores if c != root]
-    plane = [c for c in others if topo.may_write(root, c)]
     far = [c for c in others if not topo.may_write(root, c)]
-    mate = [c for c in far if topo.mates(topo.chip(root), topo.chip(c))]
-    r = [c for c in far if c not in mate]
-    ports = [c for c in range(CORES_SIMULATED) if c != root and topo.chip(c) == topo.chip(root)
-             and all(topo.may_write(c, d) for d in others)]
-    a0, a1 = [c for c in ports if topo.die(c) == topo.die(root)][:2]
-    b0, b1 = [c for c in ports if topo.die(c) != topo.die(root)][:2]
-    m, p = mate[0], plane[0]
+    p = [c for c in others if c not in far][0]
+    m = [c for c in far if topo.mates(topo.chip(root), topo.chip(c))][0]
+    r = [c for c in far if c != m]
+    home = topo.chip(root)
+
+    def ports(chip_ok, same_die):
+        return [c for c in range(CORES_SIMULATED) if c not in T.cores and chip_ok(topo.chip(c))
+                and all(topo.may_write(c, d) for d in others) and (topo.die(c) == topo.die(root)) == same_die]
+
+    def beside(d, same_die):
+        return ports(lambda k: topo.same_plane(home, k) and topo.mates(k, topo.chip(d)), same_die)[0]
+    a0, a1 = ports(lambda k: k == home, True)[:2]
+    b0, b1 = ports(lambda k: k == home, False)[:2]
+    e = beside(r[1], False)
     off = low(topo.mask(root, p), 8)
     chip = topo.mask(root, a0)
     rest = chip & ~off
     return {
-        root: [("pa", off, [a0, a1, b0, b1]), ("c0", rest, [a0, b0]), ("c1", chip, [a1, b1]),
-               ("pb", chip, [a0, b0]), ("c0", off, [p])],
-        a0: [("pa", off, [m]), ("c0", off, [m, r[0]]), ("pb", off, [r[1], r[2], p])],
-        b0: [("pa", off, [r[1]]), ("c0", off, [r[1], r[2]]), ("pb", off, [m, r[0]])],
-        a1: [("pa", off, [r[2], p]), ("c1", off, [r[1], r[2], p])],
-        b1: [("pa", off, [r[0]]), ("c1", off, [r[0], m])],
+        root: [("u0", rest, [b0, a1]), ("u1", off, [e]), ("u2", rest, [a0]), ("pl", chip, [b1, a1]),
+               ("u3", chip, [a0]), ("u2", chip, [b0]), ("u1", off, [p]), ("u3", rest, [a1]), ("u2", off, [p]),
+               ("u3", off, [p])],
+        b0: [("u0", off, [r[0], r[1], m]), ("u2", off, [r[0], r[1], m])],
+        a1: [("u0", off, [r[2], p]), ("pl", off, [r[0], m]), ("u3", off, [r[2]])],
+        e: [("u1", off, [r[2], r[0], r[1], m])],
+        a0: [("u2", off, [r[2]]), ("u3", off, [r[0], r[1], m])],
+        b1: [("pl", off, [r[2], r[1], p])],
     }
 
 
 def view(T, piece):
-    buf, a, b, last = PIECES[piece]
-    return T.hq[:, a:b].bitcast(dt.uint8) if buf == "hq" else T.hs[:, a:b]
+    buf, a, b = PIECES[piece]
+    return T.hq[:, 128 * a:128 * b].bitcast(dt.uint8) if buf == "hq" else T.hs[:, 128 * a:128 * b]
 
 
 def send(g, T, topo, calls, ready):
@@ -84,7 +95,7 @@ def send(g, T, topo, calls, ready):
     g.wait_ge(T.sem.sent, total)
 
 
-def queue(eng, sem):
+def queue(sem):
     n = [0]
 
     def do(ins):
@@ -111,10 +122,10 @@ def output(g, T, vdo, tdo, sdo, w2_ready, h_ready, free):
             g.scalar.wait_ge(S.ten, k)
             cp[u] = sdo(g.scalar.activation(dst, src, ActivationFunctionType.Copy))
     g.sync.wait_ge(S.vec, cp[0])
-    g.sync.dma_start(T.y[:, 0:128], T.yt[:, 0:128]).then_inc(S.st0, 16)
     g.sync.wait_ge(S.act, cp[1])
+    g.sync.dma_start(T.y[:, 0:256], T.yt[:, 0:256]).then_inc(S.st0, 16)
     g.sync.wait_ge(S.vec, cp[2])
-    g.sync.dma_start(T.y[:, 128:384], T.yt[:, 128:384]).then_inc(S.st1, 16)
+    g.sync.dma_start(T.y[:, 256:384], T.yt[:, 256:384]).then_inc(S.st1, 16)
     g.scalar.wait_ge(S.act, cp[3])
     g.scalar.dma_start(T.y[:, 384:512], T.yt[:, 384:512]).then_inc(S.st2, 16)
     g.sync.wait_ge(S.st0, 16)
@@ -124,60 +135,71 @@ def output(g, T, vdo, tdo, sdo, w2_ready, h_ready, free):
 
 def root_program(g, T, topo, calls):
     S = T.sem
-    vdo, tdo, sdo = queue(g.vector, S.vec), queue(g.tensor, S.ten), queue(g.scalar, S.act)
+    vdo, tdo, sdo = queue(S.vec), queue(S.ten), queue(S.act)
     g.sync.dma_start(T.xt[:, 0:512], T.x[:, 0:512]).then_inc(S.lx0, 16)
     g.scalar.dma_start(T.wt[:, 0:1024], T.w1[:, 0:1024]).then_inc(S.lw0, 16)
-    g.sync.dma_start(T.wt[:, 1024:2048], T.w1[:, 1024:2048]).then_inc(S.lw1, 16)
-    g.scalar.dma_start(T.xt[:, 512:1024], T.x[:, 512:1024]).then_inc(S.lx1, 16)
+    g.sync.dma_start(T.wt[:, 1024:1536], T.w1[:, 1024:1536]).then_inc(S.lw2, 16)
+    g.scalar.dma_start(T.wt[:, 1536:2048], T.w1[:, 1536:2048]).then_inc(S.lw3, 16)
+    g.sync.dma_start(T.xt[:, 512:1024], T.x[:, 512:1024]).then_inc(S.lx1, 16)
     g.sync.dma_start(T.xt[:, 1024:2048], T.x[:, 1024:2048]).then_inc(S.lx2, 16)
-    g.scalar.dma_start(T.w2t[:], T.w2[:]).then_inc(S.lw2, 16)
+    g.sync.dma_start(T.w2t[:], T.w2[:]).then_inc(S.lv, 16)
 
     def quant(q, s, t, k):
         return vdo(g.vector.quantize_mx(q[:, 128 * k:128 * k + 128], s[:, 128 * k:128 * k + 128],
                                         t[:, 512 * k:512 * k + 512]))
 
-    xk, wk, hk = [0] * 4, [0] * 4, [0] * 4
-    g.vector.wait_ge(S.lx0, 16)
-    xk[0] = quant(T.xq, T.xs, T.xt, 0)
-    for i in range(4):
-        if i % 2 == 0:
-            g.vector.wait_ge(S.lw1 if i else S.lw0, 16)
-        wk[i] = quant(T.wq, T.ws, T.wt, i)
+    def sides(u, i):
+        bank = 4 * (u % 2) + i
+        return T.z[:, 512 * bank:512 * bank + 128], T.h[:, 512 * u + i:512 * u + 512:4]
+    have = {}
     done = {}
-    for u in range(4):
-        if u == 1:
-            g.vector.wait_ge(S.lx1, 16)
-            xk[1] = quant(T.xq, T.xs, T.xt, 1)
-        if u == 2:
-            g.vector.wait_ge(S.lx2, 16)
-            xk[2] = quant(T.xq, T.xs, T.xt, 2)
-            xk[3] = quant(T.xq, T.xs, T.xt, 3)
-        for i in range(4):
-            bank = 4 * (u % 2) + i
-            g.tensor.wait_ge(S.vec, max(xk[u], wk[i]))
+    todo = [(u, i) for u in range(4) for i in range(4)]
+    mm = {}
+    held = []
+
+    def emptied(eng, u, i):
+        eng.wait_ge(S[done[(u, i)][0]], done[(u, i)][1])
+
+    def products():
+        while todo:
+            u, i = todo[0]
+            if "x%d" % u not in have or "w%d" % i not in have or (u >= 2 and (u - 2, i) not in done):
+                return
+            todo.pop(0)
+            g.tensor.wait_ge(S.vec, max(have["x%d" % u], have["w%d" % i]))
             if u >= 2:
-                g.tensor.wait_ge(*done[(u - 2, i)])
-            k = tdo(g.tensor.matmul_mx(T.z[:, 512 * bank:512 * bank + 128],
-                                       T.wq[:, 128 * i:128 * i + 128], T.ws[:, 128 * i:128 * i + 128],
-                                       T.xq[:, 128 * u:128 * u + 128], T.xs[:, 128 * u:128 * u + 128], True, True))
-            src = T.z[:, 512 * bank:512 * bank + 128]
-            dst = T.h[:, 512 * u + i:512 * u + 512:4]
-            if i % 2 == 0:
-                g.scalar.wait_ge(S.ten, k)
-                done[(u, i)] = (S.act, sdo(g.scalar.activation(dst, src, ActivationFunctionType.Relu, scale=C)))
-            else:
-                g.vector.wait_ge(S.ten, k)
-                done[(u, i)] = (S.vec, vdo(g.vector.tensor_scalar(dst, src, 0.0, C, AluOpType.max, AluOpType.mult)))
-        g.vector.wait_ge(*done[(u, 2)])
-        g.vector.wait_ge(*done[(u, 3)])
-        hk[u] = quant(T.hq, T.hs, T.h, u)
-    g.vector.wait_ge(S.lw2, 16)
+                emptied(g.tensor, u - 2, i)
+            src, dst = sides(u, i)
+            mm[(u, i)] = tdo(g.tensor.matmul_mx(src, T.wq[:, 128 * i:128 * i + 128], T.ws[:, 128 * i:128 * i + 128],
+                                                T.xq[:, 128 * u:128 * u + 128], T.xs[:, 128 * u:128 * u + 128],
+                                                True, True))
+            if "z%d%d" % (u, i) not in VECTOR:
+                g.scalar.wait_ge(S.ten, mm[(u, i)])
+                done[(u, i)] = ("act", sdo(g.scalar.activation(dst, src, ActivationFunctionType.Relu, scale=C)))
+
+    for step in VECTOR:
+        kind, u = step[0], int(step[1])
+        if kind in "xw":
+            if LOADED[step] not in held:
+                held.append(LOADED[step])
+                g.vector.wait_ge(S[LOADED[step]], 16)
+            have[step] = quant(T.xq, T.xs, T.xt, u) if kind == "x" else quant(T.wq, T.ws, T.wt, u)
+        elif kind == "z":
+            i = int(step[2])
+            src, dst = sides(u, i)
+            g.vector.wait_ge(S.ten, mm[(u, i)])
+            done[(u, i)] = ("vec", vdo(g.vector.tensor_scalar(dst, src, 0.0, C, AluOpType.max, AluOpType.mult)))
+        else:
+            for i in range(4):
+                emptied(g.vector, u, i)
+            have[step] = quant(T.hq, T.hs, T.h, u)
+        products()
+    g.vector.wait_ge(S.lv, 16)
     w2k = vdo(g.vector.quantize_mx(T.w2q[:, 0:128], T.w2s[:, 0:128], T.w2t[:, 0:512]))
 
-    def free(u):
-        g.tensor.wait_ge(*done[(2, u)])
-    output(g, T, vdo, tdo, sdo, w2k, lambda u: g.tensor.wait_ge(S.vec, hk[u]), free)
-    send(g, T, topo, calls, lambda piece: g.wait_ge(S.vec, hk[PIECES[piece][3]]))
+    output(g, T, vdo, tdo, sdo, w2k, lambda u: g.tensor.wait_ge(S.vec, have["h%d" % u]),
+           lambda u: emptied(g.tensor, 2, u))
+    send(g, T, topo, calls, lambda piece: g.wait_ge(S.vec, have["h%d" % (PIECES[piece][2] - 1)]))
 
 
 def rank_program(g, core, T, topo):
@@ -197,13 +219,15 @@ def rank_program(g, core, T, topo):
         send(g, T, topo, calls, lambda piece: g.wait_ge(S[piece], arrives[piece]))
     if rank is None:
         return
-    vdo, tdo, sdo = queue(g.vector, S.vec), queue(g.tensor, S.ten), queue(g.scalar, S.act)
-    g.sync.dma_start(T.w2t[:], T.w2[:]).then_inc(S.lw2, 16)
-    g.vector.wait_ge(S.lw2, 16)
+    vdo, tdo, sdo = queue(S.vec), queue(S.ten), queue(S.act)
+    g.sync.dma_start(T.w2t[:], T.w2[:]).then_inc(S.lv, 16)
+    g.vector.wait_ge(S.lv, 16)
     w2k = vdo(g.vector.quantize_mx(T.w2q[:, 0:128], T.w2s[:, 0:128], T.w2t[:, 0:512]))
-    need = [["pa", "c0"], ["pb"], ["c1"], []]
+    waited = []
 
     def h_ready(u):
-        for piece in need[u]:
-            g.tensor.wait_ge(S[piece], arrives[piece])
+        for piece in PIECES:
+            if PIECES[piece][1] <= u < PIECES[piece][2] and piece not in waited:
+                waited.append(piece)
+                g.tensor.wait_ge(S[piece], arrives[piece])
     output(g, T, vdo, tdo, sdo, w2k, h_ready, lambda u: None)

from concourse.bass import DstId, RemoteDMATransfer
from concourse.mybir import dt, AluOpType, ActivationFunctionType

SCRATCH = {
    "xt": ("sbuf", [128, 2048], "bfloat16"),
    "wt": ("sbuf", [128, 2048], "bfloat16"),
    "w2t": ("sbuf", [128, 512], "bfloat16"),
    "xq": ("sbuf", [128, 512], "float8_e4m3fn_x4"),
    "xs": ("sbuf", [128, 512], "uint8"),
    "wq": ("sbuf", [128, 512], "float8_e4m3fn_x4"),
    "ws": ("sbuf", [128, 512], "uint8"),
    "w2q": ("sbuf", [128, 128], "float8_e4m3fn_x4"),
    "w2s": ("sbuf", [128, 128], "uint8"),
    "h": ("sbuf", [128, 2048], "bfloat16"),
    "hq": ("sbuf", [128, 512], "float8_e4m3fn_x4"),
    "hs": ("sbuf", [128, 512], "uint8"),
    "yt": ("sbuf", [128, 512], "float32"),
    "z": ("psum", [128, 4096], "float32"),
}
PIECES = {"u0": ("hq", 0, 1), "u1": ("hq", 1, 2), "u2": ("hq", 2, 3), "u3": ("hq", 3, 4), "pl": ("hs", 0, 4)}
LOADED = {"x0": "lx0", "x1": "lx1", "x2": "lx2", "x3": "lx2", "w0": "lw0", "w1": "lw0", "w2": "lw2", "w3": "lw3"}
SEMAPHORES = ["lx0", "lx1", "lx2", "lw0", "lw2", "lw3", "lv", "vec", "ten", "act", "st0", "st1", "st2",
              "sent"] + list(PIECES)
VECTOR = ["x0", "w0", "w1", "w2", "w3", "z01", "x1", "z03", "h0", "x2", "x3", "z10", "z13", "h1",
          "z21", "z23", "h2", "z31", "z33", "h3"]
C = 0.019
CORES_SIMULATED = 112


def bits(mask):
    return bin(mask).count("1")


def low(mask, n):
    out = 0
    for e in range(16):
        if mask >> e & 1 and bits(out) < n:
            out |= 1 << e
    return out


def routes(T, topo):
    root = T.cores[T.root]
    others = [c for c in T.cores if c != root]
    far = [c for c in others if not topo.may_write(root, c)]
    p = [c for c in others if c not in far][0]
    m = [c for c in far if topo.mates(topo.chip(root), topo.chip(c))][0]
    r = [c for c in far if c != m]
    home = topo.chip(root)

    def ports(chip_ok, same_die):
        return [c for c in range(CORES_SIMULATED) if c not in T.cores and chip_ok(topo.chip(c))
                and all(topo.may_write(c, d) for d in others) and (topo.die(c) == topo.die(root)) == same_die]

    def beside(d, same_die):
        return ports(lambda k: topo.same_plane(home, k) and topo.mates(k, topo.chip(d)), same_die)[0]
    a0, a1 = ports(lambda k: k == home, True)[:2]
    b0, b1 = ports(lambda k: k == home, False)[:2]
    e = beside(r[1], False)
    off = low(topo.mask(root, p), 8)
    chip = topo.mask(root, a0)
    rest = chip & ~off
    return {
        root: [("u0", rest, [b0, a1]), ("u1", off, [e]), ("u2", rest, [a0]), ("pl", chip, [b1, a1]),
               ("u3", chip, [a0]), ("u2", chip, [b0]), ("u1", off, [p]), ("u3", rest, [a1]), ("u2", off, [p]),
               ("u3", off, [p])],
        b0: [("u0", off, [r[0], r[1], m]), ("u2", off, [r[0], r[1], m])],
        a1: [("u0", off, [r[2], p]), ("pl", off, [r[0], m]), ("u3", off, [r[2]])],
        e: [("u1", off, [r[2], r[0], r[1], m])],
        a0: [("u2", off, [r[2]]), ("u3", off, [r[0], r[1], m])],
        b1: [("pl", off, [r[2], r[1], p])],
    }


def view(T, piece):
    buf, a, b = PIECES[piece]
    return T.hq[:, 128 * a:128 * b].bitcast(dt.uint8) if buf == "hq" else T.hs[:, 128 * a:128 * b]


def send(g, T, topo, calls, ready):
    total = 0
    seen = []
    for piece, mask, dests in calls:
        if piece not in seen:
            seen.append(piece)
            ready(piece)
        ids = []
        for d in dests:
            rid, pid, _se = topo.addr(d)
            ids.append(DstId(rid=rid, pnc=pid))
        g.remote_dma_fused([RemoteDMATransfer(dst_ids=ids, dma_engine_mask=mask, remote_sem=T.sem[piece],
                                              srcs=[view(T, piece)], dsts=[view(T, piece) for _ in dests])],
                           local_sem=T.sem.sent)
        total += bits(mask)
    g.wait_ge(T.sem.sent, total)


def queue(sem):
    n = [0]

    def do(ins):
        n[0] += 1
        ins.then_inc(sem, 1)
        return n[0]
    return do


def output(g, T, vdo, tdo, sdo, w2_ready, h_ready, free):
    S = T.sem
    cp = [0] * 4
    g.tensor.wait_ge(S.vec, w2_ready)
    for u in range(4):
        h_ready(u)
        free(u)
        k = tdo(g.tensor.matmul_mx(T.z[:, 512 * u:512 * u + 128], T.w2q[:, 0:128], T.w2s[:, 0:128],
                                   T.hq[:, 128 * u:128 * u + 128], T.hs[:, 128 * u:128 * u + 128], True, True))
        src, dst = T.z[:, 512 * u:512 * u + 128], T.yt[:, 128 * u:128 * u + 128]
        if u % 2 == 0:
            g.vector.wait_ge(S.ten, k)
            cp[u] = vdo(g.vector.tensor_copy(dst, src))
        else:
            g.scalar.wait_ge(S.ten, k)
            cp[u] = sdo(g.scalar.activation(dst, src, ActivationFunctionType.Copy))
    g.sync.wait_ge(S.vec, cp[0])
    g.sync.wait_ge(S.act, cp[1])
    g.sync.dma_start(T.y[:, 0:256], T.yt[:, 0:256]).then_inc(S.st0, 16)
    g.sync.wait_ge(S.vec, cp[2])
    g.sync.dma_start(T.y[:, 256:384], T.yt[:, 256:384]).then_inc(S.st1, 16)
    g.scalar.wait_ge(S.act, cp[3])
    g.scalar.dma_start(T.y[:, 384:512], T.yt[:, 384:512]).then_inc(S.st2, 16)
    g.sync.wait_ge(S.st0, 16)
    g.sync.wait_ge(S.st1, 16)
    g.scalar.wait_ge(S.st2, 16)


def root_program(g, T, topo, calls):
    S = T.sem
    vdo, tdo, sdo = queue(S.vec), queue(S.ten), queue(S.act)
    g.sync.dma_start(T.xt[:, 0:512], T.x[:, 0:512]).then_inc(S.lx0, 16)
    g.scalar.dma_start(T.wt[:, 0:1024], T.w1[:, 0:1024]).then_inc(S.lw0, 16)
    g.sync.dma_start(T.wt[:, 1024:1536], T.w1[:, 1024:1536]).then_inc(S.lw2, 16)
    g.scalar.dma_start(T.wt[:, 1536:2048], T.w1[:, 1536:2048]).then_inc(S.lw3, 16)
    g.sync.dma_start(T.xt[:, 512:1024], T.x[:, 512:1024]).then_inc(S.lx1, 16)
    g.sync.dma_start(T.xt[:, 1024:2048], T.x[:, 1024:2048]).then_inc(S.lx2, 16)
    g.sync.dma_start(T.w2t[:], T.w2[:]).then_inc(S.lv, 16)

    def quant(q, s, t, k):
        return vdo(g.vector.quantize_mx(q[:, 128 * k:128 * k + 128], s[:, 128 * k:128 * k + 128],
                                        t[:, 512 * k:512 * k + 512]))

    def sides(u, i):
        bank = 4 * (u % 2) + i
        return T.z[:, 512 * bank:512 * bank + 128], T.h[:, 512 * u + i:512 * u + 512:4]
    have = {}
    done = {}
    todo = [(u, i) for u in range(4) for i in range(4)]
    mm = {}
    held = []

    def emptied(eng, u, i):
        eng.wait_ge(S[done[(u, i)][0]], done[(u, i)][1])

    def products():
        while todo:
            u, i = todo[0]
            if "x%d" % u not in have or "w%d" % i not in have or (u >= 2 and (u - 2, i) not in done):
                return
            todo.pop(0)
            g.tensor.wait_ge(S.vec, max(have["x%d" % u], have["w%d" % i]))
            if u >= 2:
                emptied(g.tensor, u - 2, i)
            src, dst = sides(u, i)
            mm[(u, i)] = tdo(g.tensor.matmul_mx(src, T.wq[:, 128 * i:128 * i + 128], T.ws[:, 128 * i:128 * i + 128],
                                                T.xq[:, 128 * u:128 * u + 128], T.xs[:, 128 * u:128 * u + 128],
                                                True, True))
            if "z%d%d" % (u, i) not in VECTOR:
                g.scalar.wait_ge(S.ten, mm[(u, i)])
                done[(u, i)] = ("act", sdo(g.scalar.activation(dst, src, ActivationFunctionType.Relu, scale=C)))

    for step in VECTOR:
        kind, u = step[0], int(step[1])
        if kind in "xw":
            if LOADED[step] not in held:
                held.append(LOADED[step])
                g.vector.wait_ge(S[LOADED[step]], 16)
            have[step] = quant(T.xq, T.xs, T.xt, u) if kind == "x" else quant(T.wq, T.ws, T.wt, u)
        elif kind == "z":
            i = int(step[2])
            src, dst = sides(u, i)
            g.vector.wait_ge(S.ten, mm[(u, i)])
            done[(u, i)] = ("vec", vdo(g.vector.tensor_scalar(dst, src, 0.0, C, AluOpType.max, AluOpType.mult)))
        else:
            for i in range(4):
                emptied(g.vector, u, i)
            have[step] = quant(T.hq, T.hs, T.h, u)
        products()
    g.vector.wait_ge(S.lv, 16)
    w2k = vdo(g.vector.quantize_mx(T.w2q[:, 0:128], T.w2s[:, 0:128], T.w2t[:, 0:512]))

    output(g, T, vdo, tdo, sdo, w2k, lambda u: g.tensor.wait_ge(S.vec, have["h%d" % u]),
           lambda u: emptied(g.tensor, 2, u))
    send(g, T, topo, calls, lambda piece: g.wait_ge(S.vec, have["h%d" % (PIECES[piece][2] - 1)]))


def rank_program(g, core, T, topo):
    R = routes(T, topo)
    rank = T.rank_of(core)
    calls = R[core] if core in R else []
    if rank is not None and rank == T.root:
        root_program(g, T, topo, calls)
        return
    S = T.sem
    arrives = {}
    for src in R:
        for piece, mask, dests in R[src]:
            if core in dests:
                arrives[piece] = bits(mask)
    if calls:
        send(g, T, topo, calls, lambda piece: g.wait_ge(S[piece], arrives[piece]))
    if rank is None:
        return
    vdo, tdo, sdo = queue(S.vec), queue(S.ten), queue(S.act)
    g.sync.dma_start(T.w2t[:], T.w2[:]).then_inc(S.lv, 16)
    g.vector.wait_ge(S.lv, 16)
    w2k = vdo(g.vector.quantize_mx(T.w2q[:, 0:128], T.w2s[:, 0:128], T.w2t[:, 0:512]))
    waited = []

    def h_ready(u):
        for piece in PIECES:
            if PIECES[piece][1] <= u < PIECES[piece][2] and piece not in waited:
                waited.append(piece)
                g.tensor.wait_ge(S[piece], arrives[piece])
    output(g, T, vdo, tdo, sdo, w2k, h_ready, lambda u: None)
